import numpy as np
import ml_dtypes


def mxq(x, axis, fmt="e4m3"):
    dtype, down = {"e4m3": (ml_dtypes.float8_e4m3fn, 7), "e5m2": (ml_dtypes.float8_e5m2, 14)}[fmt]
    v = np.moveaxis(np.asarray(x, np.float32).astype(ml_dtypes.bfloat16).astype(np.float64), axis, -1)
    blocks = v.reshape(v.shape[:-1] + (-1, 32))
    amax = np.abs(blocks).max(-1, keepdims=True)
    byte = np.maximum(np.where(amax > 0, np.frexp(amax)[1] - 1 + 127, 0) - down, 1)
    scale = np.exp2(byte - 127.0)
    codes = (blocks / scale).astype(np.float32).astype(dtype).astype(np.float64)
    return np.moveaxis((codes * scale).reshape(v.shape), -1, axis)


WIDE = False


def mx_kscale(k):
    if not WIDE:
        return np.ones(k)
    levels = np.array([10, -10, 5, -5, 0])
    if k % 512:
        return np.exp2(np.random.permutation(np.resize(levels, k // 32))).repeat(32)
    a = np.empty((k // 512, 16))
    for p in range(k // 512):
        a[p, :8] = np.random.permutation(np.resize(levels, 8))
        for g in range(8):
            far = levels[np.abs(levels - a[p, g]) >= 10]
            a[p, g + 8] = far[np.random.randint(len(far))]
    return np.exp2(a.ravel()).repeat(32)


def f64(x):
    return np.asarray(x).astype(np.float64)


def striped(idx):
    return np.tile(idx.reshape(-1, 16).T, (8, 1)).astype(np.uint16)


def unstriped(offs):
    return offs[:16].T.reshape(-1).astype(np.int64)


K, T, E, C, N = 3072, 768, 6, 256, 128


def by_expert(wq, xq):
    return np.concatenate([wq[e].T @ xq[:, e * C:(e + 1) * C] for e in range(E)], axis=1)


def setup_inputs():
    n = np.random.standard_normal
    s = mx_kscale(K)[:, None]
    first = np.random.permutation(np.repeat(np.arange(E), T // E))
    second = (first + 1 + np.random.permutation(np.repeat(np.arange(E - 1), -(-T // (E - 1)))[:T])) % E
    while np.bincount(second, minlength=E).max() != T // E:
        load = np.bincount(second, minlength=E); hi, lo = int(load.argmax()), int(load.argmin())
        t = np.flatnonzero((second == hi) & (first != lo))[0]; second[t] = lo
    slot_token = np.empty(E * C, np.int64); pos = np.empty((2, T), np.int64); fill = np.zeros(E, np.int64)
    place = np.stack([np.random.permutation(C) for _ in range(E)])
    for r, deal in enumerate((first, second)):
        for t in np.random.permutation(T):
            e = deal[t]; j = e * C + place[e, fill[e]]; fill[e] += 1; slot_token[j] = t; pos[r, t] = j
    g = np.random.uniform(0.2, 0.8, T)
    return {
        "xT": (n((K, T)) * s).astype(np.float32),
        "w": (n((E, K, N)) / np.sqrt(K) / s[None]).astype(np.float32),
        "gate": np.stack([np.tile(g, (N, 1)), np.tile(1.0 - g, (N, 1))]).astype(np.float32),
        "offs": striped(slot_token),
        "pos1": striped(pos[0]),
        "pos2": striped(pos[1]),
    }


def reference(xT, w, gate, offs, pos1, pos2):
    idx = unstriped(offs)
    xq = mxq(f64(xT)[:, idx], 0, "e4m3")
    y = by_expert(mxq(f64(w), 1, "e4m3"), xq)
    return f64(gate[0]) * y[:, unstriped(pos1)] + f64(gate[1]) * y[:, unstriped(pos2)]

@@ -1,0 +1,185 @@
+from contextlib import ExitStack
+
+import concourse.mybir as mybir
+
+K, T, E, C, N = 3072, 768, 6, 256, 128
+P = 128
+PACK = 4
+PASSES = K // (P * PACK)
+SLOTS = E * C
+FLOPS = 2 * K * N * SLOTS
+
+F32 = mybir.dt.float32
+BF16 = mybir.dt.bfloat16
+U32 = mybir.dt.uint32
+U16 = mybir.dt.uint16
+U8 = mybir.dt.uint8
+I32 = mybir.dt.int32
+FP8X4 = mybir.dt.float8_e4m3fn_x4
+MULT = mybir.AluOpType.mult
+ADD = mybir.AluOpType.add
+
+FIRST_CUTS = ((0, 256), (256, 512), (512, 768))
+CUTS = ((0, 512), (512, 768))
+LOW = (2, 3, 4, 5)
+HIGH = (0, 1)
+ORDER = (2, 3, 4, 0, 1, 5)
+CHUNKS = (4,) * 8 + (2, 2)
+LOADS = "x0 x1 x2 x3 w0 x4 w1 x5 w2 w3 w4 w5 w6 w7"
+
+
+def lay(copy, dst, src):
+    copy(
+        out=dst.rearrange("p (c i) t -> p c t i", i=4),
+        in_=src.rearrange("p t (c i) -> p c t i", i=4),
+    )
+
+
+def tile_routed_moe_kernel(tc, xT, w, gate, offs, pos1, pos2, out):
+    nc = tc.nc
+    x_rows = xT.rearrange("(a p j) t -> a p j t", p=P, j=PACK)
+    w_rows = w.rearrange("e (a p j) n -> p (e a) (j n)", p=P, j=PACK)
+
+    with ExitStack() as ctx:
+        lists = ctx.enter_context(tc.tile_pool(name="lists", bufs=1))
+        keep = ctx.enter_context(tc.tile_pool(name="keep", bufs=1))
+        xstage = ctx.enter_context(tc.tile_pool(name="xstage", bufs=3))
+        wstage = ctx.enter_context(tc.tile_pool(name="wstage", bufs=5))
+        wlaid = ctx.enter_context(tc.tile_pool(name="wlaid", bufs=5))
+        psum = ctx.enter_context(tc.psum_pool(name="psum", bufs=1))
+
+        offs_t = lists.tile([P, SLOTS // 16], U16, name="offs_t")
+        pos1_t = lists.tile([P, T // 16], U16, name="pos1_t")
+        pos2_t = lists.tile([P, T // 16], U16, name="pos2_t")
+
+        x_words = [keep.tile([P, T], U32, name=f"x_words{a}", align_bytes=64) for a in range(PASSES)]
+        g_words = [keep.tile([P, SLOTS], U32, name=f"g_words{a}", align_bytes=64) for a in range(4)]
+        x_low = keep.tile([P, T], U8, name="x_low", align_bytes=64)
+        x_high = keep.tile([P, T], U8, name="x_high", align_bytes=64)
+        place = {}
+        for i, a in enumerate(LOW):
+            place[a] = (0, PACK * i)
+        for i, a in enumerate(HIGH):
+            place[a] = (1, PACK * i)
+        all_bytes = keep.tile([P, T], U8, name="all_bytes", tag="turn", align_bytes=64)
+        g_bytes = keep.tile([P, SLOTS], U8, name="g_bytes", align_bytes=64)
+        g_high = keep.tile([P, SLOTS], U8, name="g_high", align_bytes=64)
+        gates = keep.tile([P, 2, T], F32, name="gates")
+        y = keep.tile([P, SLOTS], F32, name="y")
+        term1 = keep.tile([P, T], F32, name="term1")
+        term2 = keep.tile([P, T], F32, name="term2")
+
+        for tile in (x_high, x_low, all_bytes, g_high):
+            nc.gpsimd.memset(tile[:], 0)
+
+        first_unit = [sum(CHUNKS[:c]) for c in range(len(CHUNKS))]
+        w_raw, x_raw = {}, {}
+
+        def load_w(c):
+            units = CHUNKS[c]
+            raw = wstage.tile([P, units, PACK, N], F32, name=f"w_raw{units}", bufs=4 if units == 4 else 2)
+            nc.sync.dma_start(
+                out=raw[:].rearrange("p u j n -> p u (j n)"),
+                in_=w_rows[:, first_unit[c] : first_unit[c] + units, :],
+            )
+            w_raw[c] = raw
+
+        def load_x(a):
+            raw = xstage.tile([P, PACK, T], F32, name="x_raw")
+            for t0, t1 in ((0, 512), (512, 768)) if a == 0 else ((0, T),):
+                nc.sync.dma_start(out=raw[:, :, t0:t1], in_=x_rows[a, :, :, t0:t1])
+            x_raw[a] = raw
+
+        w_codes = {}
+
+        def do_w(c, copy):
+            units = CHUNKS[c]
+            laid = wlaid.tile([P, units * N, PACK], BF16, name=f"w_laid{units}", align_bytes=64, bufs=5 if units == 4 else 2)
+            raw = w_raw[c]
+            copy(
+                out=laid[:].rearrange("p (u c i) t -> p u c t i", u=units, i=4),
+                in_=raw[:].rearrange("p u t (c i) -> p u c t i", i=4),
+            )
+            words = keep.tile([P, units * N], U32, name=f"w_words{c}", align_bytes=64)
+            scales = keep.tile([P, units * N], U8, name=f"w_scales{c}", align_bytes=64)
+            nc.vector.quantize_mx(
+                out=words[:].bitcast(FP8X4), scales=scales[:], in_=laid[:].rearrange("p w t -> p (w t)")
+            )
+            for u in range(units):
+                w_codes[first_unit[c] + u] = (
+                    words[:, u * N : (u + 1) * N],
+                    scales[:, u * N : (u + 1) * N],
+                )
+
+        def quantize_x(a, cuts, copies):
+            plane, row = place[a]
+            for (t0, t1), copy in zip(cuts, copies):
+                laid = xstage.tile([P, t1 - t0, PACK], BF16, name=f"x_laid{t1 - t0}", align_bytes=64)
+                lay(copy, laid[:], x_raw[a][:, :, t0:t1])
+                nc.vector.quantize_mx(
+                    out=x_words[a][:, t0:t1].bitcast(FP8X4),
+                    scales=(x_low, x_high)[plane][row:P, t0:t1],
+                    in_=laid[:].rearrange("p w t -> p (w t)"),
+                )
+
+        def gather(out, window, cuts):
+            for s0, s1 in zip(cuts, cuts[1:]):
+                nc.vector.tensor_copy(out=out[:, s0:s1], in_=window[:].indirect(offs_t[:, s0 // 16 : s1 // 16]))
+
+        nc.sync.dma_start(offs_t[:], offs)
+        for step in LOADS.split():
+            (load_x if step[0] == "x" else load_w)(int(step[1:]))
+        nc.sync.dma_start(pos1_t[:], pos1)
+        nc.sync.dma_start(pos2_t[:], pos2)
+        nc.sync.dma_start(out=gates[:], in_=gate.rearrange("g p t -> p g t"))
+        for c in range(8, len(CHUNKS)):
+            load_w(c)
+
+        vcopy, scopy = nc.vector.tensor_copy, nc.scalar.copy
+        even = (0, 512, 1024, 1536)
+        quantize_x(0, FIRST_CUTS, (vcopy, scopy, vcopy))
+        quantize_x(1, CUTS, (scopy, vcopy))
+        for q in range(0, P, 32):
+            nc.sync.dma_start(out=all_bytes[q + 16 : q + 24, :].bitcast(I32), in_=x_high[q : q + 8, :].bitcast(I32))
+        gather(g_words[0], x_words[0], even)
+        quantize_x(2, CUTS, (scopy, scopy))
+        gather(g_words[1], x_words[1], even)
+        quantize_x(3, CUTS, (scopy, scopy))
+        gather(g_words[2], x_words[2], even)
+        do_w(0, scopy)
+        quantize_x(4, CUTS, (scopy, scopy))
+        do_w(1, scopy)
+        quantize_x(5, CUTS, (scopy, scopy))
+        for q in range(0, P, 32):
+            nc.vector.tensor_copy(out=all_bytes[q : q + 16, :].bitcast(I32), in_=x_low[q : q + 16, :].bitcast(I32))
+        for c in range(2, len(CHUNKS)):
+            do_w(c, vcopy if c == len(CHUNKS) - 1 else scopy)
+        gather(g_bytes, all_bytes, even)
+        for q in range(0, P, 32):
+            nc.sync.dma_start(out=g_high[q : q + 8, :].bitcast(I32), in_=g_bytes[q + 16 : q + 24, :].bitcast(I32))
+        gather(g_words[3], x_words[3], even)
+        g_late = keep.tile([P, 2, SLOTS], U32, name="g_late", tag="turn", align_bytes=64)
+        g_words += [g_late[:, 0, :], g_late[:, 1, :]]
+        gather(g_words[4], x_words[4], even)
+        gather(g_words[5], x_words[5], (0, 512, 1024, 1280, 1536))
+
+        for e in range(E):
+            acc = psum.tile([N, C], F32, name=f"acc{e}")
+            mine = slice(e * C, (e + 1) * C)
+            for a in ORDER:
+                words, scales = w_codes[e * PASSES + a]
+                nc.tensor.matmul_mx(
+                    out=acc[:],
+                    lhsT=words.bitcast(FP8X4),
+                    lhsT_scale=scales,
+                    rhs=g_words[a][:, mine].bitcast(FP8X4),
+                    rhs_scale=(g_bytes, g_high)[place[a][0]][place[a][1] : P, mine],
+                    start=(a == ORDER[0]),
+                    stop=(a == ORDER[-1]),
+                )
+            scopy(out=y[:, mine], in_=acc[:])
+
+        nc.vector.tensor_tensor(term1[:], y[:].indirect(pos1_t[:]), gates[:, 0, :], MULT)
+        nc.vector.tensor_tensor(term2[:], y[:].indirect(pos2_t[:]), gates[:, 1, :], MULT)
+        nc.vector.tensor_tensor(term1[:], term1[:], term2[:], ADD)
+        nc.sync.dma_start(out=out, in_=term1[:])

@@ -24,8 +24,7 @@ CUTS = ((0, 512), (512, 768))
 LOW = (2, 3, 4, 5)
 HIGH = (0, 1)
 ORDER = (2, 3, 4, 0, 1, 5)
-CHUNKS = (4,) * 8 + (2, 2)
-LOADS = "x0 x1 x2 x3 w0 x4 w1 x5 w2 w3 w4 w5 w6 w7"
+RING = 5
 
 
 def lay(copy, dst, src):
@@ -43,9 +42,9 @@ def tile_routed_moe_kernel(tc, xT, w, gate, offs, pos1, pos2, out):
     with ExitStack() as ctx:
         lists = ctx.enter_context(tc.tile_pool(name="lists", bufs=1))
         keep = ctx.enter_context(tc.tile_pool(name="keep", bufs=1))
-        xstage = ctx.enter_context(tc.tile_pool(name="xstage", bufs=3))
-        wstage = ctx.enter_context(tc.tile_pool(name="wstage", bufs=5))
-        wlaid = ctx.enter_context(tc.tile_pool(name="wlaid", bufs=5))
+        ring = ctx.enter_context(tc.tile_pool(name="ring", bufs=RING))
+        xlaid = ctx.enter_context(tc.tile_pool(name="xlaid", bufs=3))
+        wlaid = ctx.enter_context(tc.tile_pool(name="wlaid", bufs=4))
         psum = ctx.enter_context(tc.psum_pool(name="psum", bufs=1))
 
         offs_t = lists.tile([P, SLOTS // 16], U16, name="offs_t")
@@ -53,7 +52,7 @@ def tile_routed_moe_kernel(tc, xT, w, gate, offs, pos1, pos2, out):
         pos2_t = lists.tile([P, T // 16], U16, name="pos2_t")
 
         x_words = [keep.tile([P, T], U32, name=f"x_words{a}", align_bytes=64) for a in range(PASSES)]
-        g_words = [keep.tile([P, SLOTS], U32, name=f"g_words{a}", align_bytes=64) for a in range(4)]
+        g_words = [keep.tile([P, SLOTS], U32, name=f"g_words{a}", align_bytes=64) for a in range(PASSES)]
         x_low = keep.tile([P, T], U8, name="x_low", align_bytes=64)
         x_high = keep.tile([P, T], U8, name="x_high", align_bytes=64)
         place = {}
@@ -61,7 +60,7 @@ def tile_routed_moe_kernel(tc, xT, w, gate, offs, pos1, pos2, out):
             place[a] = (0, PACK * i)
         for i, a in enumerate(HIGH):
             place[a] = (1, PACK * i)
-        all_bytes = keep.tile([P, T], U8, name="all_bytes", tag="turn", align_bytes=64)
+        all_bytes = keep.tile([P, T], U8, name="all_bytes", align_bytes=64)
         g_bytes = keep.tile([P, SLOTS], U8, name="g_bytes", align_bytes=64)
         g_high = keep.tile([P, SLOTS], U8, name="g_high", align_bytes=64)
         gates = keep.tile([P, 2, T], F32, name="gates")
@@ -72,49 +71,46 @@ def tile_routed_moe_kernel(tc, xT, w, gate, offs, pos1, pos2, out):
         for tile in (x_high, x_low, all_bytes, g_high):
             nc.gpsimd.memset(tile[:], 0)
 
-        first_unit = [sum(CHUNKS[:c]) for c in range(len(CHUNKS))]
         w_raw, x_raw = {}, {}
 
-        def load_w(c):
-            units = CHUNKS[c]
-            raw = wstage.tile([P, units, PACK, N], F32, name=f"w_raw{units}", bufs=4 if units == 4 else 2)
-            nc.sync.dma_start(
-                out=raw[:].rearrange("p u j n -> p u (j n)"),
-                in_=w_rows[:, first_unit[c] : first_unit[c] + units, :],
-            )
-            w_raw[c] = raw
+        def load_w(e):
+            raw = ring.tile([P, PASSES, PACK, N], F32, name=f"w_raw{e}", tag="raw")
+            for u0, u1 in ((0, 4), (4, 6)) if e == E - 1 else ((0, 6),):
+                nc.sync.dma_start(
+                    out=raw[:, u0:u1].rearrange("p u j n -> p u (j n)"),
+                    in_=w_rows[:, e * PASSES + u0 : e * PASSES + u1, :],
+                )
+            w_raw[e] = raw
 
         def load_x(a):
-            raw = xstage.tile([P, PACK, T], F32, name="x_raw")
+            raw = ring.tile([P, PACK, T], F32, name=f"x_raw{a}", tag="raw")
             for t0, t1 in ((0, 512), (512, 768)) if a == 0 else ((0, T),):
                 nc.sync.dma_start(out=raw[:, :, t0:t1], in_=x_rows[a, :, :, t0:t1])
             x_raw[a] = raw
 
         w_codes = {}
 
-        def do_w(c, copy):
-            units = CHUNKS[c]
-            laid = wlaid.tile([P, units * N, PACK], BF16, name=f"w_laid{units}", align_bytes=64, bufs=5 if units == 4 else 2)
-            raw = w_raw[c]
-            copy(
-                out=laid[:].rearrange("p (u c i) t -> p u c t i", u=units, i=4),
-                in_=raw[:].rearrange("p u t (c i) -> p u c t i", i=4),
-            )
-            words = keep.tile([P, units * N], U32, name=f"w_words{c}", align_bytes=64)
-            scales = keep.tile([P, units * N], U8, name=f"w_scales{c}", align_bytes=64)
-            nc.vector.quantize_mx(
-                out=words[:].bitcast(FP8X4), scales=scales[:], in_=laid[:].rearrange("p w t -> p (w t)")
-            )
-            for u in range(units):
-                w_codes[first_unit[c] + u] = (
-                    words[:, u * N : (u + 1) * N],
-                    scales[:, u * N : (u + 1) * N],
+        def quantize_w(e, copies):
+            for (u0, u1), copy in zip(((0, 4), (4, 6)), copies):
+                units = u1 - u0
+                laid = wlaid.tile([P, units * N, PACK], BF16, name=f"w_laid{e}_{u0}", tag=f"w_laid{units}", align_bytes=64)
+                copy(
+                    out=laid[:].rearrange("p (u c i) t -> p u c t i", u=units, i=4),
+                    in_=w_raw[e][:, u0:u1].rearrange("p u t (c i) -> p u c t i", i=4),
                 )
+                words = keep.tile([P, units * N], U32, name=f"w_words{e}_{u0}", align_bytes=64)
+                scales = keep.tile([P, units * N], U8, name=f"w_scales{e}_{u0}", align_bytes=64)
+                nc.vector.quantize_mx(
+                    out=words[:].bitcast(FP8X4), scales=scales[:], in_=laid[:].rearrange("p w t -> p (w t)")
+                )
+                for u in range(units):
+                    cols = slice(u * N, (u + 1) * N)
+                    w_codes[e, u0 + u] = (words[:, cols], scales[:, cols])
 
         def quantize_x(a, cuts, copies):
             plane, row = place[a]
             for (t0, t1), copy in zip(cuts, copies):
-                laid = xstage.tile([P, t1 - t0, PACK], BF16, name=f"x_laid{t1 - t0}", align_bytes=64)
+                laid = xlaid.tile([P, t1 - t0, PACK], BF16, name=f"x_laid{t1 - t0}", align_bytes=64)
                 lay(copy, laid[:], x_raw[a][:, :, t0:t1])
                 nc.vector.quantize_mx(
                     out=x_words[a][:, t0:t1].bitcast(FP8X4),
@@ -127,39 +123,44 @@ def tile_routed_moe_kernel(tc, xT, w, gate, offs, pos1, pos2, out):
                 nc.vector.tensor_copy(out=out[:, s0:s1], in_=window[:].indirect(offs_t[:, s0 // 16 : s1 // 16]))
 
         nc.sync.dma_start(offs_t[:], offs)
-        for step in LOADS.split():
-            (load_x if step[0] == "x" else load_w)(int(step[1:]))
-        nc.sync.dma_start(pos1_t[:], pos1)
-        nc.sync.dma_start(pos2_t[:], pos2)
-        nc.sync.dma_start(out=gates[:], in_=gate.rearrange("g p t -> p g t"))
-        for c in range(8, len(CHUNKS)):
-            load_w(c)
-
+        load_x(0)
+        load_x(1)
+        load_x(2)
+        load_x(3)
         vcopy, scopy = nc.vector.tensor_copy, nc.scalar.copy
         even = (0, 512, 1024, 1536)
         quantize_x(0, FIRST_CUTS, (vcopy, scopy, vcopy))
         quantize_x(1, CUTS, (scopy, vcopy))
         for q in range(0, P, 32):
             nc.sync.dma_start(out=all_bytes[q + 16 : q + 24, :].bitcast(I32), in_=x_high[q : q + 8, :].bitcast(I32))
+        load_w(0)
+        load_x(4)
         gather(g_words[0], x_words[0], even)
         quantize_x(2, CUTS, (scopy, scopy))
+        load_x(5)
         gather(g_words[1], x_words[1], even)
         quantize_x(3, CUTS, (scopy, scopy))
+        load_w(1)
         gather(g_words[2], x_words[2], even)
-        do_w(0, scopy)
+        quantize_w(0, (scopy, scopy))
+        load_w(2)
         quantize_x(4, CUTS, (scopy, scopy))
-        do_w(1, scopy)
+        load_w(3)
         quantize_x(5, CUTS, (scopy, scopy))
         for q in range(0, P, 32):
             nc.vector.tensor_copy(out=all_bytes[q : q + 16, :].bitcast(I32), in_=x_low[q : q + 16, :].bitcast(I32))
-        for c in range(2, len(CHUNKS)):
-            do_w(c, vcopy if c == len(CHUNKS) - 1 else scopy)
         gather(g_bytes, all_bytes, even)
         for q in range(0, P, 32):
             nc.sync.dma_start(out=g_high[q : q + 8, :].bitcast(I32), in_=g_bytes[q + 16 : q + 24, :].bitcast(I32))
+        nc.sync.dma_start(pos1_t[:], pos1)
+        nc.sync.dma_start(pos2_t[:], pos2)
+        load_w(4)
+        quantize_w(1, (scopy, scopy))
+        nc.sync.dma_start(out=gates[:], in_=gate.rearrange("g p t -> p g t"))
+        load_w(5)
+        for e in range(2, E):
+            quantize_w(e, (scopy, vcopy if e == E - 1 else scopy))
         gather(g_words[3], x_words[3], even)
-        g_late = keep.tile([P, 2, SLOTS], U32, name="g_late", tag="turn", align_bytes=64)
-        g_words += [g_late[:, 0, :], g_late[:, 1, :]]
         gather(g_words[4], x_words[4], even)
         gather(g_words[5], x_words[5], (0, 512, 1024, 1280, 1536))
 
@@ -167,7 +168,7 @@ def tile_routed_moe_kernel(tc, xT, w, gate, offs, pos1, pos2, out):
             acc = psum.tile([N, C], F32, name=f"acc{e}")
             mine = slice(e * C, (e + 1) * C)
             for a in ORDER:
-                words, scales = w_codes[e * PASSES + a]
+                words, scales = w_codes[e, a]
                 nc.tensor.matmul_mx(
                     out=acc[:],
                     lhsT=words.bitcast(FP8X4),

@@ -19,19 +19,12 @@ FP8X4 = mybir.dt.float8_e4m3fn_x4
 MULT = mybir.AluOpType.mult
 ADD = mybir.AluOpType.add
 
-FIRST_CUTS = ((0, 256), (256, 512), (512, 768))
+THIRDS = ((0, 256), (256, 512), (512, 768))
 CUTS = ((0, 512), (512, 768))
 LOW = (2, 3, 4, 5)
 HIGH = (0, 1)
 ORDER = (2, 3, 4, 0, 1, 5)
 RING = 5
-
-
-def lay(copy, dst, src):
-    copy(
-        out=dst.rearrange("p (c i) t -> p c t i", i=4),
-        in_=src.rearrange("p t (c i) -> p c t i", i=4),
-    )
 
 
 def tile_routed_moe_kernel(tc, xT, w, gate, offs, pos1, pos2, out):
@@ -43,8 +36,8 @@ def tile_routed_moe_kernel(tc, xT, w, gate, offs, pos1, pos2, out):
         lists = ctx.enter_context(tc.tile_pool(name="lists", bufs=1))
         keep = ctx.enter_context(tc.tile_pool(name="keep", bufs=1))
         ring = ctx.enter_context(tc.tile_pool(name="ring", bufs=RING))
-        xlaid = ctx.enter_context(tc.tile_pool(name="xlaid", bufs=3))
-        wlaid = ctx.enter_context(tc.tile_pool(name="wlaid", bufs=4))
+        laid_ring = ctx.enter_context(tc.tile_pool(name="laid_ring", bufs=4))
+        pair_ring = ctx.enter_context(tc.tile_pool(name="pair_ring", bufs=2))
         psum = ctx.enter_context(tc.psum_pool(name="psum", bufs=1))
 
         offs_t = lists.tile([P, SLOTS // 16], U16, name="offs_t")
@@ -63,7 +56,6 @@ def tile_routed_moe_kernel(tc, xT, w, gate, offs, pos1, pos2, out):
         all_bytes = keep.tile([P, T], U8, name="all_bytes", align_bytes=64)
         g_bytes = keep.tile([P, SLOTS], U8, name="g_bytes", align_bytes=64)
         g_high = keep.tile([P, SLOTS], U8, name="g_high", align_bytes=64)
-        gates = keep.tile([P, 2, T], F32, name="gates")
         y = keep.tile([P, SLOTS], F32, name="y")
         term1 = keep.tile([P, T], F32, name="term1")
         term2 = keep.tile([P, T], F32, name="term2")
@@ -72,81 +64,101 @@ def tile_routed_moe_kernel(tc, xT, w, gate, offs, pos1, pos2, out):
             nc.gpsimd.memset(tile[:], 0)
 
         w_raw, x_raw = {}, {}
+        tenants = []
+
+        def raw_tile(shape, name):
+            queue = nc.sync if len(tenants) < RING else nc.scalar
+            tenants.append(name)
+            return ring.tile(shape, F32, name=name, tag="raw"), queue
 
         def load_w(e):
-            raw = ring.tile([P, PASSES, PACK, N], F32, name=f"w_raw{e}", tag="raw")
+            raw, queue = raw_tile([P, PASSES, PACK, N], f"w_raw{e}")
             for u0, u1 in ((0, 4), (4, 6)) if e == E - 1 else ((0, 6),):
-                nc.sync.dma_start(
+                queue.dma_start(
                     out=raw[:, u0:u1].rearrange("p u j n -> p u (j n)"),
                     in_=w_rows[:, e * PASSES + u0 : e * PASSES + u1, :],
                 )
             w_raw[e] = raw
 
         def load_x(a):
-            raw = ring.tile([P, PACK, T], F32, name=f"x_raw{a}", tag="raw")
-            for t0, t1 in ((0, 512), (512, 768)) if a == 0 else ((0, T),):
-                nc.sync.dma_start(out=raw[:, :, t0:t1], in_=x_rows[a, :, :, t0:t1])
+            raw, queue = raw_tile([P, PACK, T], f"x_raw{a}")
+            for t0, t1 in THIRDS if a == 0 else ((0, T),):
+                queue.dma_start(out=raw[:, :, t0:t1], in_=x_rows[a, :, :, t0:t1])
             x_raw[a] = raw
 
+        vcopy, scopy = nc.vector.tensor_copy, nc.scalar.copy
         w_codes = {}
 
-        def quantize_w(e, copies):
-            for (u0, u1), copy in zip(((0, 4), (4, 6)), copies):
-                units = u1 - u0
-                laid = wlaid.tile([P, units * N, PACK], BF16, name=f"w_laid{e}_{u0}", tag=f"w_laid{units}", align_bytes=64)
+        def lay_w(e, lays, laid, first):
+            for u0, u1, copy in lays:
                 copy(
-                    out=laid[:].rearrange("p (u c i) t -> p u c t i", u=units, i=4),
+                    out=laid[:, (first + u0) * N : (first + u1) * N, :].rearrange("p (u c i) t -> p u c t i", u=u1 - u0, i=4),
                     in_=w_raw[e][:, u0:u1].rearrange("p u t (c i) -> p u c t i", i=4),
                 )
-                words = keep.tile([P, units * N], U32, name=f"w_words{e}_{u0}", align_bytes=64)
-                scales = keep.tile([P, units * N], U8, name=f"w_scales{e}_{u0}", align_bytes=64)
-                nc.vector.quantize_mx(
-                    out=words[:].bitcast(FP8X4), scales=scales[:], in_=laid[:].rearrange("p w t -> p (w t)")
-                )
-                for u in range(units):
-                    cols = slice(u * N, (u + 1) * N)
-                    w_codes[e, u0 + u] = (words[:, cols], scales[:, cols])
 
-        def quantize_x(a, cuts, copies):
+        def pair_tile(e):
+            return pair_ring.tile([P, 2 * PASSES * N, PACK], BF16, name=f"w_laid{e}", tag="pair", align_bytes=64)
+
+        def quantize_w(e, cuts, laid):
+            width = cuts[-1][1] * N
+            words = keep.tile([P, width], U32, name=f"w_words{e}", align_bytes=64)
+            scales = keep.tile([P, width], U8, name=f"w_scales{e}", align_bytes=64)
+            for u0, u1 in cuts:
+                cols = slice(u0 * N, u1 * N)
+                nc.vector.quantize_mx(
+                    out=words[:, cols].bitcast(FP8X4),
+                    scales=scales[:, cols],
+                    in_=laid[:, cols, :].rearrange("p w t -> p (w t)"),
+                )
+            for u in range(cuts[-1][1]):
+                cols = slice(u * N, (u + 1) * N)
+                w_codes[e + u // PASSES, u % PASSES] = (words[:, cols], scales[:, cols])
+
+        def quantize_x(a, cuts, lays):
             plane, row = place[a]
-            for (t0, t1), copy in zip(cuts, copies):
-                laid = xlaid.tile([P, t1 - t0, PACK], BF16, name=f"x_laid{t1 - t0}", align_bytes=64)
-                lay(copy, laid[:], x_raw[a][:, :, t0:t1])
+            laid = laid_ring.tile([P, T, PACK], BF16, name=f"x_laid{a}", tag="laid", align_bytes=64)
+            for t0, t1, copy in lays:
+                copy(
+                    out=laid[:, t0:t1, :].rearrange("p (c i) t -> p c t i", i=4),
+                    in_=x_raw[a][:, :, t0:t1].rearrange("p t (c i) -> p c t i", i=4),
+                )
+            for t0, t1 in cuts:
                 nc.vector.quantize_mx(
                     out=x_words[a][:, t0:t1].bitcast(FP8X4),
                     scales=(x_low, x_high)[plane][row:P, t0:t1],
-                    in_=laid[:].rearrange("p w t -> p (w t)"),
+                    in_=laid[:, t0:t1, :].rearrange("p w t -> p (w t)"),
                 )
 
         def gather(out, window, cuts):
             for s0, s1 in zip(cuts, cuts[1:]):
                 nc.vector.tensor_copy(out=out[:, s0:s1], in_=window[:].indirect(offs_t[:, s0 // 16 : s1 // 16]))
 
+        even = (0, 512, 1024, 1536)
+        whole = ((0, PASSES, scopy),)
         nc.sync.dma_start(offs_t[:], offs)
         load_x(0)
         load_x(1)
         load_x(2)
         load_x(3)
-        vcopy, scopy = nc.vector.tensor_copy, nc.scalar.copy
-        even = (0, 512, 1024, 1536)
-        quantize_x(0, FIRST_CUTS, (vcopy, scopy, vcopy))
-        quantize_x(1, CUTS, (scopy, vcopy))
+        quantize_x(0, THIRDS, ((0, 256, vcopy), (256, 512, scopy), (512, 768, vcopy),))
+        quantize_x(1, CUTS, ((0, 512, scopy), (512, 768, vcopy),))
         for q in range(0, P, 32):
             nc.sync.dma_start(out=all_bytes[q + 16 : q + 24, :].bitcast(I32), in_=x_high[q : q + 8, :].bitcast(I32))
         load_w(0)
         load_x(4)
         gather(g_words[0], x_words[0], even)
-        quantize_x(2, CUTS, (scopy, scopy))
+        quantize_x(2, CUTS, ((0, T, scopy),))
         load_x(5)
         gather(g_words[1], x_words[1], even)
-        quantize_x(3, CUTS, (scopy, scopy))
+        quantize_x(3, CUTS, ((0, T, scopy),))
         load_w(1)
         gather(g_words[2], x_words[2], even)
-        quantize_w(0, (scopy, scopy))
+        laid01 = pair_tile(0)
+        lay_w(0, whole, laid01, 0)
         load_w(2)
-        quantize_x(4, CUTS, (scopy, scopy))
+        quantize_x(4, CUTS, ((0, T, scopy),))
         load_w(3)
-        quantize_x(5, CUTS, (scopy, scopy))
+        quantize_x(5, CUTS, ((0, T, scopy),))
         for q in range(0, P, 32):
             nc.vector.tensor_copy(out=all_bytes[q : q + 16, :].bitcast(I32), in_=x_low[q : q + 16, :].bitcast(I32))
         gather(g_bytes, all_bytes, even)
@@ -155,11 +167,19 @@ def tile_routed_moe_kernel(tc, xT, w, gate, offs, pos1, pos2, out):
         nc.sync.dma_start(pos1_t[:], pos1)
         nc.sync.dma_start(pos2_t[:], pos2)
         load_w(4)
-        quantize_w(1, (scopy, scopy))
-        nc.sync.dma_start(out=gates[:], in_=gate.rearrange("g p t -> p g t"))
+        lay_w(1, whole, laid01, PASSES)
+        quantize_w(0, ((0, 8), (8, 12)), laid01)
+        gates, queue = raw_tile([P, 2, T], "gates")
+        queue.dma_start(out=gates[:], in_=gate.rearrange("g p t -> p g t"))
         load_w(5)
-        for e in range(2, E):
-            quantize_w(e, (scopy, vcopy if e == E - 1 else scopy))
+        laid23 = pair_tile(2)
+        lay_w(2, whole, laid23, 0)
+        lay_w(3, whole, laid23, PASSES)
+        quantize_w(2, ((0, 8), (8, 12)), laid23)
+        laid45 = pair_tile(4)
+        lay_w(4, whole, laid45, 0)
+        lay_w(5, ((0, 2, scopy), (2, 4, scopy), (4, 6, vcopy)), laid45, PASSES)
+        quantize_w(4, ((0, 4), (4, 8), (8, 10), (10, 12)), laid45)
         gather(g_words[3], x_words[3], even)
         gather(g_words[4], x_words[4], even)
         gather(g_words[5], x_words[5], (0, 512, 1024, 1280, 1536))
@@ -178,7 +198,7 @@ def tile_routed_moe_kernel(tc, xT, w, gate, offs, pos1, pos2, out):
                     start=(a == ORDER[0]),
                     stop=(a == ORDER[-1]),
                 )
-            scopy(out=y[:, mine], in_=acc[:])
+            (vcopy if e == E - 1 else scopy)(out=y[:, mine], in_=acc[:])
 
         nc.vector.tensor_tensor(term1[:], y[:].indirect(pos1_t[:]), gates[:, 0, :], MULT)
         nc.vector.tensor_tensor(term2[:], y[:].indirect(pos2_t[:]), gates[:, 1, :], MULT)

@@ -19,7 +19,6 @@ FP8X4 = mybir.dt.float8_e4m3fn_x4
 MULT = mybir.AluOpType.mult
 ADD = mybir.AluOpType.add
 
-THIRDS = ((0, 256), (256, 512), (512, 768))
 CUTS = ((0, 512), (512, 768))
 LOW = (2, 3, 4, 5)
 HIGH = (0, 1)
@@ -82,8 +81,7 @@ def tile_routed_moe_kernel(tc, xT, w, gate, offs, pos1, pos2, out):
 
         def load_x(a):
             raw, queue = raw_tile([P, PACK, T], f"x_raw{a}")
-            for t0, t1 in THIRDS if a == 0 else ((0, T),):
-                queue.dma_start(out=raw[:, :, t0:t1], in_=x_rows[a, :, :, t0:t1])
+            queue.dma_start(out=raw[:], in_=x_rows[a])
             x_raw[a] = raw
 
         vcopy, scopy = nc.vector.tensor_copy, nc.scalar.copy
@@ -140,7 +138,7 @@ def tile_routed_moe_kernel(tc, xT, w, gate, offs, pos1, pos2, out):
         load_x(1)
         load_x(2)
         load_x(3)
-        quantize_x(0, THIRDS, ((0, 256, vcopy), (256, 512, scopy), (512, 768, vcopy),))
+        quantize_x(0, CUTS, ((0, 256, vcopy), (256, 512, scopy), (512, 768, vcopy),))
         quantize_x(1, CUTS, ((0, 512, scopy), (512, 768, vcopy),))
         for q in range(0, P, 32):
             nc.sync.dma_start(out=all_bytes[q + 16 : q + 24, :].bitcast(I32), in_=x_high[q : q + 8, :].bitcast(I32))
@@ -169,9 +167,9 @@ def tile_routed_moe_kernel(tc, xT, w, gate, offs, pos1, pos2, out):
         load_w(4)
         lay_w(1, whole, laid01, PASSES)
         quantize_w(0, ((0, 8), (8, 12)), laid01)
+        load_w(5)
         gates, queue = raw_tile([P, 2, T], "gates")
         queue.dma_start(out=gates[:], in_=gate.rearrange("g p t -> p g t"))
-        load_w(5)
         laid23 = pair_tile(2)
         lay_w(2, whole, laid23, 0)
         lay_w(3, whole, laid23, PASSES)
@@ -201,6 +199,14 @@ def tile_routed_moe_kernel(tc, xT, w, gate, offs, pos1, pos2, out):
             (vcopy if e == E - 1 else scopy)(out=y[:, mine], in_=acc[:])
 
         nc.vector.tensor_tensor(term1[:], y[:].indirect(pos1_t[:]), gates[:, 0, :], MULT)
-        nc.vector.tensor_tensor(term2[:], y[:].indirect(pos2_t[:]), gates[:, 1, :], MULT)
-        nc.vector.tensor_tensor(term1[:], term1[:], term2[:], ADD)
-        nc.sync.dma_start(out=out, in_=term1[:])
+        halves = (slice(0, T // 2), slice(T // 2, T))
+        for half in halves:
+            nc.vector.tensor_tensor(
+                term2[:, half],
+                y[:].indirect(pos2_t[:, half.start // 16 : half.stop // 16]),
+                gates[:, 1, half],
+                MULT,
+            )
+        for half in halves:
+            nc.vector.tensor_tensor(term1[:, half], term1[:, half], term2[:, half], ADD)
+            nc.sync.dma_start(out=out[:, half], in_=term1[:, half])

from contextlib import ExitStack

import concourse.mybir as mybir

K, T, E, C, N = 3072, 768, 6, 256, 128
P = 128
PACK = 4
PASSES = K // (P * PACK)
SLOTS = E * C
FLOPS = 2 * K * N * SLOTS

F32 = mybir.dt.float32
BF16 = mybir.dt.bfloat16
U32 = mybir.dt.uint32
U16 = mybir.dt.uint16
U8 = mybir.dt.uint8
I32 = mybir.dt.int32
FP8X4 = mybir.dt.float8_e4m3fn_x4
MULT = mybir.AluOpType.mult
ADD = mybir.AluOpType.add

CUTS = ((0, 512), (512, 768))
LOW = (2, 3, 4, 5)
HIGH = (0, 1)
ORDER = (2, 3, 4, 0, 1, 5)
RING = 5


def tile_routed_moe_kernel(tc, xT, w, gate, offs, pos1, pos2, out):
    nc = tc.nc
    x_rows = xT.rearrange("(a p j) t -> a p j t", p=P, j=PACK)
    w_rows = w.rearrange("e (a p j) n -> p (e a) (j n)", p=P, j=PACK)

    with ExitStack() as ctx:
        lists = ctx.enter_context(tc.tile_pool(name="lists", bufs=1))
        keep = ctx.enter_context(tc.tile_pool(name="keep", bufs=1))
        ring = ctx.enter_context(tc.tile_pool(name="ring", bufs=RING))
        laid_ring = ctx.enter_context(tc.tile_pool(name="laid_ring", bufs=4))
        pair_ring = ctx.enter_context(tc.tile_pool(name="pair_ring", bufs=2))
        psum = ctx.enter_context(tc.psum_pool(name="psum", bufs=1))

        offs_t = lists.tile([P, SLOTS // 16], U16, name="offs_t")
        pos1_t = lists.tile([P, T // 16], U16, name="pos1_t")
        pos2_t = lists.tile([P, T // 16], U16, name="pos2_t")

        x_words = [keep.tile([P, T], U32, name=f"x_words{a}", align_bytes=64) for a in range(PASSES)]
        g_words = [keep.tile([P, SLOTS], U32, name=f"g_words{a}", align_bytes=64) for a in range(PASSES)]
        x_low = keep.tile([P, T], U8, name="x_low", align_bytes=64)
        x_high = keep.tile([P, T], U8, name="x_high", align_bytes=64)
        place = {}
        for i, a in enumerate(LOW):
            place[a] = (0, PACK * i)
        for i, a in enumerate(HIGH):
            place[a] = (1, PACK * i)
        all_bytes = keep.tile([P, T], U8, name="all_bytes", align_bytes=64)
        g_bytes = keep.tile([P, SLOTS], U8, name="g_bytes", align_bytes=64)
        g_high = keep.tile([P, SLOTS], U8, name="g_high", align_bytes=64)
        y = keep.tile([P, SLOTS], F32, name="y")
        term1 = keep.tile([P, T], F32, name="term1")
        term2 = keep.tile([P, T], F32, name="term2")

        for tile in (x_high, x_low, all_bytes, g_high):
            nc.gpsimd.memset(tile[:], 0)

        w_raw, x_raw = {}, {}
        tenants = []

        def raw_tile(shape, name):
            queue = nc.sync if len(tenants) < RING else nc.scalar
            tenants.append(name)
            return ring.tile(shape, F32, name=name, tag="raw"), queue

        def load_w(e):
            raw, queue = raw_tile([P, PASSES, PACK, N], f"w_raw{e}")
            for u0, u1 in ((0, 4), (4, 6)) if e == E - 1 else ((0, 6),):
                queue.dma_start(
                    out=raw[:, u0:u1].rearrange("p u j n -> p u (j n)"),
                    in_=w_rows[:, e * PASSES + u0 : e * PASSES + u1, :],
                )
            w_raw[e] = raw

        def load_x(a):
            raw, queue = raw_tile([P, PACK, T], f"x_raw{a}")
            queue.dma_start(out=raw[:], in_=x_rows[a])
            x_raw[a] = raw

        vcopy, scopy = nc.vector.tensor_copy, nc.scalar.copy
        w_codes = {}

        def lay_w(e, lays, laid, first):
            for u0, u1, copy in lays:
                copy(
                    out=laid[:, (first + u0) * N : (first + u1) * N, :].rearrange("p (u c i) t -> p u c t i", u=u1 - u0, i=4),
                    in_=w_raw[e][:, u0:u1].rearrange("p u t (c i) -> p u c t i", i=4),
                )

        def pair_tile(e):
            return pair_ring.tile([P, 2 * PASSES * N, PACK], BF16, name=f"w_laid{e}", tag="pair", align_bytes=64)

        def quantize_w(e, cuts, laid):
            width = cuts[-1][1] * N
            words = keep.tile([P, width], U32, name=f"w_words{e}", align_bytes=64)
            scales = keep.tile([P, width], U8, name=f"w_scales{e}", align_bytes=64)
            for u0, u1 in cuts:
                cols = slice(u0 * N, u1 * N)
                nc.vector.quantize_mx(
                    out=words[:, cols].bitcast(FP8X4),
                    scales=scales[:, cols],
                    in_=laid[:, cols, :].rearrange("p w t -> p (w t)"),
                )
            for u in range(cuts[-1][1]):
                cols = slice(u * N, (u + 1) * N)
                w_codes[e + u // PASSES, u % PASSES] = (words[:, cols], scales[:, cols])

        def quantize_x(a, cuts, lays):
            plane, row = place[a]
            laid = laid_ring.tile([P, T, PACK], BF16, name=f"x_laid{a}", tag="laid", align_bytes=64)
            for t0, t1, copy in lays:
                copy(
                    out=laid[:, t0:t1, :].rearrange("p (c i) t -> p c t i", i=4),
                    in_=x_raw[a][:, :, t0:t1].rearrange("p t (c i) -> p c t i", i=4),
                )
            for t0, t1 in cuts:
                nc.vector.quantize_mx(
                    out=x_words[a][:, t0:t1].bitcast(FP8X4),
                    scales=(x_low, x_high)[plane][row:P, t0:t1],
                    in_=laid[:, t0:t1, :].rearrange("p w t -> p (w t)"),
                )

        def gather(out, window, cuts):
            for s0, s1 in zip(cuts, cuts[1:]):
                nc.vector.tensor_copy(out=out[:, s0:s1], in_=window[:].indirect(offs_t[:, s0 // 16 : s1 // 16]))

        even = (0, 512, 1024, 1536)
        whole = ((0, PASSES, scopy),)
        nc.sync.dma_start(offs_t[:], offs)
        load_x(0)
        load_x(1)
        load_x(2)
        load_x(3)
        quantize_x(0, CUTS, ((0, 256, vcopy), (256, 512, scopy), (512, 768, vcopy),))
        quantize_x(1, CUTS, ((0, 512, scopy), (512, 768, vcopy),))
        for q in range(0, P, 32):
            nc.sync.dma_start(out=all_bytes[q + 16 : q + 24, :].bitcast(I32), in_=x_high[q : q + 8, :].bitcast(I32))
        load_w(0)
        load_x(4)
        gather(g_words[0], x_words[0], even)
        quantize_x(2, CUTS, ((0, T, scopy),))
        load_x(5)
        gather(g_words[1], x_words[1], even)
        quantize_x(3, CUTS, ((0, T, scopy),))
        load_w(1)
        gather(g_words[2], x_words[2], even)
        laid01 = pair_tile(0)
        lay_w(0, whole, laid01, 0)
        load_w(2)
        quantize_x(4, CUTS, ((0, T, scopy),))
        load_w(3)
        quantize_x(5, CUTS, ((0, T, scopy),))
        for q in range(0, P, 32):
            nc.vector.tensor_copy(out=all_bytes[q : q + 16, :].bitcast(I32), in_=x_low[q : q + 16, :].bitcast(I32))
        gather(g_bytes, all_bytes, even)
        for q in range(0, P, 32):
            nc.sync.dma_start(out=g_high[q : q + 8, :].bitcast(I32), in_=g_bytes[q + 16 : q + 24, :].bitcast(I32))
        nc.sync.dma_start(pos1_t[:], pos1)
        nc.sync.dma_start(pos2_t[:], pos2)
        load_w(4)
        lay_w(1, whole, laid01, PASSES)
        quantize_w(0, ((0, 8), (8, 12)), laid01)
        load_w(5)
        gates, queue = raw_tile([P, 2, T], "gates")
        queue.dma_start(out=gates[:], in_=gate.rearrange("g p t -> p g t"))
        laid23 = pair_tile(2)
        lay_w(2, whole, laid23, 0)
        lay_w(3, whole, laid23, PASSES)
        quantize_w(2, ((0, 8), (8, 12)), laid23)
        laid45 = pair_tile(4)
        lay_w(4, whole, laid45, 0)
        lay_w(5, ((0, 2, scopy), (2, 4, scopy), (4, 6, vcopy)), laid45, PASSES)
        quantize_w(4, ((0, 4), (4, 8), (8, 10), (10, 12)), laid45)
        gather(g_words[3], x_words[3], even)
        gather(g_words[4], x_words[4], even)
        gather(g_words[5], x_words[5], (0, 512, 1024, 1280, 1536))

        for e in range(E):
            acc = psum.tile([N, C], F32, name=f"acc{e}")
            mine = slice(e * C, (e + 1) * C)
            for a in ORDER:
                words, scales = w_codes[e, a]
                nc.tensor.matmul_mx(
                    out=acc[:],
                    lhsT=words.bitcast(FP8X4),
                    lhsT_scale=scales,
                    rhs=g_words[a][:, mine].bitcast(FP8X4),
                    rhs_scale=(g_bytes, g_high)[place[a][0]][place[a][1] : P, mine],
                    start=(a == ORDER[0]),
                    stop=(a == ORDER[-1]),
                )
            (vcopy if e == E - 1 else scopy)(out=y[:, mine], in_=acc[:])

        nc.vector.tensor_tensor(term1[:], y[:].indirect(pos1_t[:]), gates[:, 0, :], MULT)
        halves = (slice(0, T // 2), slice(T // 2, T))
        for half in halves:
            nc.vector.tensor_tensor(
                term2[:, half],
                y[:].indirect(pos2_t[:, half.start // 16 : half.stop // 16]),
                gates[:, 1, half],
                MULT,
            )
        for half in halves:
            nc.vector.tensor_tensor(term1[:, half], term1[:, half], term2[:, half], ADD)
            nc.sync.dma_start(out=out[:, half], in_=term1[:, half])
